import numpy as np
import ml_dtypes


def mxq(x, axis, fmt="e4m3"):
    dtype, down = {"e4m3": (ml_dtypes.float8_e4m3fn, 7), "e5m2": (ml_dtypes.float8_e5m2, 14)}[fmt]
    v = np.moveaxis(np.asarray(x, np.float32).astype(ml_dtypes.bfloat16).astype(np.float64), axis, -1)
    blocks = v.reshape(v.shape[:-1] + (-1, 32))
    amax = np.abs(blocks).max(-1, keepdims=True)
    byte = np.maximum(np.where(amax > 0, np.frexp(amax)[1] - 1 + 127, 0) - down, 1)
    scale = np.exp2(byte - 127.0)
    codes = (blocks / scale).astype(np.float32).astype(dtype).astype(np.float64)
    return np.moveaxis((codes * scale).reshape(v.shape), -1, axis)


WIDE = False


def mx_kscale(k):
    if not WIDE:
        return np.ones(k)
    levels = np.array([10, -10, 5, -5, 0])
    if k % 512:
        return np.exp2(np.random.permutation(np.resize(levels, k // 32))).repeat(32)
    a = np.empty((k // 512, 16))
    for p in range(k // 512):
        a[p, :8] = np.random.permutation(np.resize(levels, 8))
        for g in range(8):
            far = levels[np.abs(levels - a[p, g]) >= 10]
            a[p, g + 8] = far[np.random.randint(len(far))]
    return np.exp2(a.ravel()).repeat(32)


def f64(x):
    return np.asarray(x).astype(np.float64)


def striped(idx):
    return np.tile(np.asarray(idx).reshape(-1, 16).T, (8, 1)).astype(np.uint16)


def unstriped(offs):
    return offs[:16].T.reshape(-1).astype(np.int64)


def sigmoid(v):
    return 1.0 / (1.0 + np.exp(-v))


D, T, I, Q, E, M = 512, 2048, 512, 512, 512, 1024


def setup_inputs():
    n = np.random.standard_normal
    idx = np.random.permutation(T)[:I]
    idx2 = np.random.permutation(T)[:I]
    idx3 = np.random.permutation(T)[:I]
    idx4 = np.random.permutation(M)[:I]
    fd = mx_kscale(D)
    fq = mx_kscale(Q)
    return {
        "query": (n((D, Q)) * 1.0 / np.sqrt(D) * fd[:, None]).astype(np.float32),
        "keys": (n((D, T)) / fd[:, None]).astype(np.float32),
        "qs": (np.random.uniform(0.5, 2.0, (Q, 1)) * fq[:, None]).astype(np.float32),
        "msgs": (n((Q, E)) * 1 / np.sqrt(Q) / fq[:, None]).astype(np.float32),
        "old": (n((E, M)) * 1.0).astype(np.float32),
        "fade": (np.random.uniform(0.3, 0.9, (1, M))).astype(np.float32),
        "offs": striped(idx),
        "offs2": striped(idx2),
        "offs3": striped(idx3),
        "offs4": striped(idx4),
    }


def reference(query, keys, qs, msgs, old, fade, offs, offs2, offs3, offs4):
    idx = unstriped(offs)
    idx2 = unstriped(offs2)
    idx3 = unstriped(offs3)
    idx4 = unstriped(offs4)
    lo3 = np.minimum(f64(keys)[:, idx], f64(keys)[:, idx2])
    hi3 = np.maximum(f64(keys)[:, idx], f64(keys)[:, idx2])
    zk = np.maximum(lo3, np.minimum(hi3, f64(keys)[:, idx3]))
    queryq = mxq(f64(query), 0, "e4m3")
    zkq = mxq(zk, 0, "e4m3")
    s = queryq.T @ zkq
    w = sigmoid(s)
    wq = w * f64(qs)
    msgsq = mxq(f64(msgs), 0, "e4m3")
    wqq = mxq(wq, 0, "e4m3")
    dl = msgsq.T @ wqq
    df = np.zeros((E, M))
    df[:, idx4] = dl
    y = f64(old) * f64(fade) + df
    return y

@@ -1,0 +1,209 @@
+from contextlib import ExitStack
+
+import concourse.mybir as mybir
+
+D, T, I, Q, E, M = 512, 2048, 512, 512, 512, 1024
+FLOPS = 2 * D * Q * I + 2 * Q * E * I
+
+F32 = mybir.dt.float32
+BF16 = mybir.dt.bfloat16
+U32 = mybir.dt.uint32
+U16 = mybir.dt.uint16
+U8 = mybir.dt.uint8
+FP8X4 = mybir.dt.float8_e4m3fn_x4
+ALU = mybir.AluOpType
+ACT = mybir.ActivationFunctionType
+
+P = 128
+PACK = 4
+HALF = I // 2
+LIST_COLS = HALF // 16
+RUN = 4
+
+
+def tile_attend_keymiddle_delivered_lean_kernel(tc, query, keys, qs, msgs, old, fade, offs, offs2, offs3, offs4, out):
+    nc = tc.nc
+    with ExitStack() as ctx:
+        held = ctx.enter_context(tc.tile_pool(name="held", bufs=1))
+        psum = ctx.enter_context(tc.psum_pool(name="psum", bufs=1))
+
+        def sb(name, shape, dtype, tag=None):
+            return held.tile(shape, dtype, name=name, tag=tag or name, align_bytes=64)
+
+        lists = [held.tile([P, I // 16], U16, name="list%d" % n) for n in range(4)]
+        key_planes = [sb("keys%d" % t, [P, T], F32) for t in range(PACK)]
+        keys_by_plane = keys.rearrange("(p t) n -> t p n", t=PACK)
+        fade_all = sb("fade_all", [P, M], F32)
+        query_raw = sb("query_raw", [P, PACK, Q], F32)
+        msgs_raw = sb("msgs_raw", [P, PACK, E], F32)
+        qs_rows = sb("qs_rows", [P, PACK], F32)
+        contents = [sb("contents%d" % j, [P, M], F32) for j in range(E // P)]
+
+        nc.sync.dma_start(out=key_planes[0][:], in_=keys_by_plane[0])
+        for n, src in enumerate((offs, offs2, offs3)):
+            nc.sync.dma_start(lists[n][:], src)
+        for t in range(1, PACK):
+            nc.sync.dma_start(out=key_planes[t][:], in_=keys_by_plane[t])
+        nc.sync.dma_start(out=query_raw[:], in_=query.rearrange("(p t) q -> p t q", t=PACK))
+        nc.sync.dma_start(out=msgs_raw[:], in_=msgs.rearrange("(p r) e -> p r e", r=PACK))
+        nc.sync.dma_start(out=qs_rows[:], in_=qs.rearrange("(p r) o -> p (r o)", r=PACK))
+        nc.sync.dma_start(lists[3][:], offs4)
+        nc.sync.dma_start(out=fade_all[:], in_=fade[0].partition_broadcast(P))
+        for j in range(E // P):
+            nc.sync.dma_start(out=contents[j][:], in_=old[j * P : (j + 1) * P, :])
+
+        delivered = [sb("delivered%d" % j, [P, M], F32) for j in range(E // P)]
+        for j in range(E // P):
+            nc.vector.memset(delivered[j][:], 0.0)
+
+        low = sb("low", [P, PACK, I], F32)
+        capped = sb("capped", [P, PACK, I], F32)
+
+        def gather(on_vector, n, t, lo, hi, got):
+            window = key_planes[t][:].indirect(lists[n][:, lo // 16 : hi // 16])
+            if on_vector:
+                nc.vector.tensor_copy(got, window)
+            else:
+                nc.scalar.activation(got, window, ACT.Copy)
+
+        def narrow(t, lo, hi, a, b, c):
+            high = sb("high%d_%d" % (t, lo), [P, hi - lo], F32)
+            nc.vector.tensor_tensor(high[:], a, b, ALU.max)
+            nc.vector.tensor_tensor(low[:, t, lo:hi], a, b, ALU.min)
+            nc.vector.tensor_tensor(capped[:, t, lo:hi], high[:], c, ALU.min)
+
+        def quantize(name, grouped, width):
+            codes = sb(name + "_codes", [P, width], U32)
+            scales = sb(name + "_scales", [P, width], U8)
+            nc.vector.quantize_mx(out=codes[:].bitcast(FP8X4), scales=scales[:], in_=grouped)
+            return codes, scales
+
+        def middle(h):
+            slots = slice(h * HALF, (h + 1) * HALF)
+            zk = sb("zk%d" % h, [P, HALF * PACK], BF16)
+            nc.vector.tensor_tensor(
+                zk[:].rearrange("p (c i t) -> p c t i", i=RUN, t=PACK),
+                low[:, :, slots].rearrange("p t (c i) -> p c t i", i=RUN),
+                capped[:, :, slots].rearrange("p t (c i) -> p c t i", i=RUN),
+                ALU.max,
+            )
+            return quantize("zk%d" % h, zk[:], HALF)
+
+        def scores(h, zk_mx, query_mx):
+            weights = sb("weights%d" % h, [P, HALF * PACK], F32)
+            for u in range(2):
+                bank = psum.tile([P, PACK, P], F32, name="score_bank%d_%d" % (h, u))
+                cols = slice(u * P, (u + 1) * P)
+                for r in range(PACK):
+                    rows = slice(r * P, (r + 1) * P)
+                    nc.tensor.matmul_mx(
+                        out=bank[:, r, :],
+                        lhsT=query_mx[0][:, rows].bitcast(FP8X4),
+                        lhsT_scale=query_mx[1][:, rows],
+                        rhs=zk_mx[0][:, cols].bitcast(FP8X4),
+                        rhs_scale=zk_mx[1][:, cols],
+                        start=True,
+                        stop=True,
+                    )
+                nc.scalar.activation(
+                    weights[:, u * P * PACK : (u + 1) * P * PACK].rearrange("p (n r) -> p n r", r=PACK),
+                    bank[:].rearrange("p r n -> p n r"),
+                    ACT.Sigmoid,
+                )
+            return weights
+
+        def weigh(h, weights):
+            wq = sb("wq%d" % h, [P, HALF * PACK], BF16)
+            nc.vector.tensor_tensor(
+                wq[:].rearrange("p (n r) -> p n r", r=PACK),
+                weights[:].rearrange("p (n r) -> p n r", r=PACK),
+                qs_rows[:].unsqueeze(1).to_broadcast([P, HALF, PACK]),
+                ALU.mult,
+            )
+            return quantize("wq%d" % h, wq[:], HALF)
+
+        def carry(h, wq_mx, msgs_mx):
+            sums = []
+            for u in range(2):
+                bank = psum.tile([P, 2, HALF], F32, name="sum_bank%d_%d" % (h, u))
+                for jj in range(2):
+                    rows = slice(jj * P, (jj + 1) * P)
+                    nc.tensor.matmul_mx(
+                        out=bank[:, jj, :],
+                        lhsT=msgs_mx[u][0][:, rows].bitcast(FP8X4),
+                        lhsT_scale=msgs_mx[u][1][:, rows],
+                        rhs=wq_mx[0][:].bitcast(FP8X4),
+                        rhs_scale=wq_mx[1][:],
+                        start=True,
+                        stop=True,
+                    )
+                dl = sb("dl%d_%d" % (h, u), [P, 2, HALF], F32)
+                nc.scalar.copy(out=dl[:], in_=bank[:])
+                sums.append(dl)
+            return sums
+
+        def deliver(on_vector, h, j, sums):
+            window = delivered[j][:].indirect(lists[3][:, h * LIST_COLS : (h + 1) * LIST_COLS])
+            src = sums[j // 2][:, j % 2, :]
+            if on_vector:
+                nc.vector.tensor_copy(window, src)
+            else:
+                nc.scalar.activation(window, src, ACT.Copy)
+
+        last = PACK - 1
+        for t in range(last):
+            got = [sb("got%d_%d" % (t, n), [P, I], F32) for n in range(3)]
+            gather(False, 0, t, 0, I, got[0][:])
+            gather(t == 0, 1, t, 0, I, got[1][:])
+            gather(True, 2, t, 0, I, got[2][:])
+            narrow(t, 0, I, got[0][:], got[1][:], got[2][:])
+        third = sb("third", [P, I], F32)
+        pair_a = sb("pair_a", [P, 2, HALF], F32)
+        gather(False, 0, last, 0, HALF, pair_a[:, 0, :])
+        gather(False, 1, last, 0, HALF, pair_a[:, 1, :])
+        gather(True, 2, last, 0, I, third[:])
+        narrow(last, 0, HALF, pair_a[:, 0, :], pair_a[:, 1, :], third[:, :HALF])
+        zk_a = middle(0)
+
+        query_grouped = sb("query_grouped", [P, Q * PACK], BF16, tag="grouped")
+        nc.scalar.copy(
+            out=query_grouped[:].rearrange("p (r m t) -> p m t r", r=PACK, t=PACK),
+            in_=query_raw[:].rearrange("p t (m r) -> p m t r", r=PACK),
+        )
+        query_mx = quantize("query", query_grouped[:], Q)
+        weights_a = scores(0, zk_a, query_mx)
+
+        pair_b = sb("pair_b", [P, 2, HALF], F32, tag="query_raw")
+        gather(False, 0, last, HALF, I, pair_b[:, 0, :])
+        gather(False, 1, last, HALF, I, pair_b[:, 1, :])
+        narrow(last, HALF, I, pair_b[:, 0, :], pair_b[:, 1, :], third[:, HALF:])
+        zk_b = middle(1)
+        wq_a = weigh(0, weights_a)
+        weights_b = scores(1, zk_b, query_mx)
+
+        msgs_grouped = sb("msgs_grouped", [P, E * PACK], BF16, tag="grouped")
+        msgs_mx = []
+        for u in range(2):
+            for jj in range(2):
+                j = 2 * u + jj
+                nc.scalar.copy(
+                    out=msgs_grouped[:, j * P * PACK : (j + 1) * P * PACK].rearrange("p (c i r) -> p c r i", i=RUN, r=PACK),
+                    in_=msgs_raw[:, :, j * P : (j + 1) * P].rearrange("p r (c i) -> p c r i", i=RUN),
+                )
+            msgs_mx.append(quantize("msgs%d" % u, msgs_grouped[:, u * 2 * P * PACK : (u + 1) * 2 * P * PACK], 2 * P))
+        sums_a = carry(0, wq_a, msgs_mx)
+        wq_b = weigh(1, weights_b)
+        sums_b = carry(1, wq_b, msgs_mx)
+        for j in range(E // P):
+            deliver(j == 0, 0, j, sums_a)
+        faded = []
+        for j, tag in enumerate(("grouped", "wq1", "weights1", "weights0")):
+            faded.append(sb("faded%d" % j, [P, M], F32, tag=tag))
+            nc.vector.tensor_tensor(faded[j][:], contents[j][:], fade_all[:], ALU.mult)
+        for j in range(E // P):
+            deliver(j == 0, 1, j, sums_b)
+            pieces = 2 if j == E // P - 1 else 1
+            for u in range(pieces):
+                cols = slice(u * M // pieces, (u + 1) * M // pieces)
+                nc.vector.tensor_tensor(contents[j][:, cols], faded[j][:, cols], delivered[j][:, cols], ALU.add)
+                nc.sync.dma_start(out=out[j * P : (j + 1) * P, cols], in_=contents[j][:, cols])

@@ -17,7 +17,6 @@ ACT = mybir.ActivationFunctionType
 P = 128
 PACK = 4
 HALF = I // 2
-LIST_COLS = HALF // 16
 RUN = 4
 
 
@@ -34,7 +33,8 @@ def tile_attend_keymiddle_delivered_lean_kernel(tc, query, keys, qs, msgs, old, 
         key_planes = [sb("keys%d" % t, [P, T], F32) for t in range(PACK)]
         keys_by_plane = keys.rearrange("(p t) n -> t p n", t=PACK)
         fade_all = sb("fade_all", [P, M], F32)
-        query_raw = sb("query_raw", [P, PACK, Q], F32)
+        query_raw = [sb("query_raw%d" % u, [P, PACK, Q // 2], F32) for u in range(2)]
+        query_by_row = query.rearrange("(p t) q -> p t q", t=PACK)
         msgs_raw = sb("msgs_raw", [P, PACK, E], F32)
         qs_rows = sb("qs_rows", [P, PACK], F32)
         contents = [sb("contents%d" % j, [P, M], F32) for j in range(E // P)]
@@ -44,7 +44,9 @@ def tile_attend_keymiddle_delivered_lean_kernel(tc, query, keys, qs, msgs, old, 
             nc.sync.dma_start(lists[n][:], src)
         for t in range(1, PACK):
             nc.sync.dma_start(out=key_planes[t][:], in_=keys_by_plane[t])
-        nc.sync.dma_start(out=query_raw[:], in_=query.rearrange("(p t) q -> p t q", t=PACK))
+            if t >= 2:
+                u = t - 2
+                nc.sync.dma_start(out=query_raw[u][:], in_=query_by_row[:, :, u * Q // 2 : (u + 1) * Q // 2])
         nc.sync.dma_start(out=msgs_raw[:], in_=msgs.rearrange("(p r) e -> p r e", r=PACK))
         nc.sync.dma_start(out=qs_rows[:], in_=qs.rearrange("(p r) o -> p (r o)", r=PACK))
         nc.sync.dma_start(lists[3][:], offs4)
@@ -112,18 +114,21 @@ def tile_attend_keymiddle_delivered_lean_kernel(tc, query, keys, qs, msgs, old, 
                 )
             return weights
 
-        def weigh(h, weights):
+        def weigh(h, weights, pieces):
             wq = sb("wq%d" % h, [P, HALF * PACK], BF16)
-            nc.vector.tensor_tensor(
-                wq[:].rearrange("p (n r) -> p n r", r=PACK),
-                weights[:].rearrange("p (n r) -> p n r", r=PACK),
-                qs_rows[:].unsqueeze(1).to_broadcast([P, HALF, PACK]),
-                ALU.mult,
-            )
+            width = HALF // pieces
+            for u in range(pieces):
+                cols = slice(u * width * PACK, (u + 1) * width * PACK)
+                nc.vector.tensor_tensor(
+                    wq[:, cols].rearrange("p (n r) -> p n r", r=PACK),
+                    weights[:, cols].rearrange("p (n r) -> p n r", r=PACK),
+                    qs_rows[:].unsqueeze(1).to_broadcast([P, width, PACK]),
+                    ALU.mult,
+                )
             return quantize("wq%d" % h, wq[:], HALF)
 
         def carry(h, wq_mx, msgs_mx):
-            sums = []
+            banks = []
             for u in range(2):
                 bank = psum.tile([P, 2, HALF], F32, name="sum_bank%d_%d" % (h, u))
                 for jj in range(2):
@@ -137,14 +142,11 @@ def tile_attend_keymiddle_delivered_lean_kernel(tc, query, keys, qs, msgs, old, 
                         start=True,
                         stop=True,
                     )
-                dl = sb("dl%d_%d" % (h, u), [P, 2, HALF], F32)
-                nc.scalar.copy(out=dl[:], in_=bank[:])
-                sums.append(dl)
-            return sums
+                banks.append(bank)
+            return banks
 
-        def deliver(on_vector, h, j, sums):
-            window = delivered[j][:].indirect(lists[3][:, h * LIST_COLS : (h + 1) * LIST_COLS])
-            src = sums[j // 2][:, j % 2, :]
+        def deliver(on_vector, j, lo, hi, src):
+            window = delivered[j][:].indirect(lists[3][:, lo // 16 : hi // 16])
             if on_vector:
                 nc.vector.tensor_copy(window, src)
             else:
@@ -154,56 +156,72 @@ def tile_attend_keymiddle_delivered_lean_kernel(tc, query, keys, qs, msgs, old, 
         for t in range(last):
             got = [sb("got%d_%d" % (t, n), [P, I], F32) for n in range(3)]
             gather(False, 0, t, 0, I, got[0][:])
-            gather(t == 0, 1, t, 0, I, got[1][:])
+            gather(t != 1, 1, t, 0, I, got[1][:])
             gather(True, 2, t, 0, I, got[2][:])
             narrow(t, 0, I, got[0][:], got[1][:], got[2][:])
-        third = sb("third", [P, I], F32)
-        pair_a = sb("pair_a", [P, 2, HALF], F32)
-        gather(False, 0, last, 0, HALF, pair_a[:, 0, :])
-        gather(False, 1, last, 0, HALF, pair_a[:, 1, :])
-        gather(True, 2, last, 0, I, third[:])
-        narrow(last, 0, HALF, pair_a[:, 0, :], pair_a[:, 1, :], third[:, :HALF])
-        zk_a = middle(0)
 
-        query_grouped = sb("query_grouped", [P, Q * PACK], BF16, tag="grouped")
-        nc.scalar.copy(
-            out=query_grouped[:].rearrange("p (r m t) -> p m t r", r=PACK, t=PACK),
-            in_=query_raw[:].rearrange("p t (m r) -> p m t r", r=PACK),
-        )
+        def last_plane(h):
+            got = [sb("got%d_%d_%d" % (last, n, h), [P, HALF], F32) for n in range(3)]
+            for n in range(3):
+                gather(False, n, last, h * HALF, (h + 1) * HALF, got[n][:])
+            narrow(last, h * HALF, (h + 1) * HALF, got[0][:], got[1][:], got[2][:])
+            return middle(h)
+
+        zk_a = last_plane(0)
+        query_grouped = sb("query_grouped", [P, Q * PACK], BF16)
+        for u in range(2):
+            nc.scalar.copy(
+                out=query_grouped[:].rearrange("p (r u m t) -> p u m t r", r=PACK, u=2, t=PACK)[:, u],
+                in_=query_raw[u][:].rearrange("p t (m r) -> p m t r", r=PACK),
+            )
         query_mx = quantize("query", query_grouped[:], Q)
         weights_a = scores(0, zk_a, query_mx)
-
-        pair_b = sb("pair_b", [P, 2, HALF], F32, tag="query_raw")
-        gather(False, 0, last, HALF, I, pair_b[:, 0, :])
-        gather(False, 1, last, HALF, I, pair_b[:, 1, :])
-        narrow(last, HALF, I, pair_b[:, 0, :], pair_b[:, 1, :], third[:, HALF:])
-        zk_b = middle(1)
-        wq_a = weigh(0, weights_a)
+        zk_b = last_plane(1)
+        wq_a = weigh(0, weights_a, 2)
         weights_b = scores(1, zk_b, query_mx)
 
-        msgs_grouped = sb("msgs_grouped", [P, E * PACK], BF16, tag="grouped")
         msgs_mx = []
-        for u in range(2):
+        for u, tag in enumerate((None, "zk0_codes")):
+            msgs_grouped = sb("msgs_grouped%d" % u, [P, 2 * P * PACK], BF16, tag=tag)
             for jj in range(2):
                 j = 2 * u + jj
                 nc.scalar.copy(
-                    out=msgs_grouped[:, j * P * PACK : (j + 1) * P * PACK].rearrange("p (c i r) -> p c r i", i=RUN, r=PACK),
+                    out=msgs_grouped[:, jj * P * PACK : (jj + 1) * P * PACK].rearrange("p (c i r) -> p c r i", i=RUN, r=PACK),
                     in_=msgs_raw[:, :, j * P : (j + 1) * P].rearrange("p r (c i) -> p c r i", i=RUN),
                 )
-            msgs_mx.append(quantize("msgs%d" % u, msgs_grouped[:, u * 2 * P * PACK : (u + 1) * 2 * P * PACK], 2 * P))
-        sums_a = carry(0, wq_a, msgs_mx)
-        wq_b = weigh(1, weights_b)
-        sums_b = carry(1, wq_b, msgs_mx)
-        for j in range(E // P):
-            deliver(j == 0, 0, j, sums_a)
-        faded = []
-        for j, tag in enumerate(("grouped", "wq1", "weights1", "weights0")):
-            faded.append(sb("faded%d" % j, [P, M], F32, tag=tag))
-            nc.vector.tensor_tensor(faded[j][:], contents[j][:], fade_all[:], ALU.mult)
-        for j in range(E // P):
-            deliver(j == 0, 1, j, sums_b)
-            pieces = 2 if j == E // P - 1 else 1
+            msgs_mx.append(quantize("msgs%d" % u, msgs_grouped[:], 2 * P))
+
+        sums0 = sb("sums0", [P, I], F32)
+        banks_a = carry(0, wq_a, msgs_mx)
+        sums1_a = sb("sums1_a", [P, HALF], F32)
+        sums23_a = sb("sums23_a", [P, 2, HALF], F32)
+        nc.scalar.copy(out=sums1_a[:], in_=banks_a[0][:, 1, :])
+        nc.scalar.copy(out=sums0[:, :HALF], in_=banks_a[0][:, 0, :])
+        nc.scalar.copy(out=sums23_a[:], in_=banks_a[1][:])
+        wq_b = weigh(1, weights_b, 1)
+        banks_b = carry(1, wq_b, msgs_mx)
+        sums1_b = sb("sums1_b", [P, HALF], F32)
+        sums23_b = sb("sums23_b", [P, 2, HALF], F32)
+        nc.vector.tensor_copy(out=sums0[:, HALF:], in_=banks_b[0][:, 0, :])
+        nc.vector.tensor_copy(out=sums1_b[:], in_=banks_b[0][:, 1, :])
+        nc.vector.tensor_copy(out=sums23_b[:], in_=banks_b[1][:])
+        deliver(False, 1, 0, HALF, sums1_a[:])
+        deliver(False, 0, 0, 128, sums0[:, :128])
+        for jj in range(2):
+            deliver(False, 2 + jj, 0, HALF, sums23_a[:, jj, :])
+        deliver(True, 0, 128, I, sums0[:, 128:])
+        deliver(False, 1, HALF, I, sums1_b[:])
+        for jj in range(2):
+            deliver(False, 2 + jj, HALF, I, sums23_b[:, jj, :])
+
+        fade_tags = ("weights0", "weights1", "sums0", "wq1_codes")
+        result_tags = (None, "weights0", None, None)
+        for j, pieces in enumerate((1, 1, 2, 4)):
+            faded = sb("faded%d" % j, [P, M], F32, tag=fade_tags[j])
+            engine = nc.vector
+            engine.tensor_tensor(faded[:], contents[j][:], fade_all[:], ALU.mult)
+            result = sb("result%d" % j, [P, M], F32, tag=result_tags[j])
             for u in range(pieces):
                 cols = slice(u * M // pieces, (u + 1) * M // pieces)
-                nc.vector.tensor_tensor(contents[j][:, cols], faded[j][:, cols], delivered[j][:, cols], ALU.add)
-                nc.sync.dma_start(out=out[j * P : (j + 1) * P, cols], in_=contents[j][:, cols])
+                nc.vector.tensor_tensor(result[:, cols], faded[:, cols], delivered[j][:, cols], ALU.add)
+                nc.sync.dma_start(out=out[j * P : (j + 1) * P, cols], in_=result[:, cols])

@@ -1,6 +1,7 @@
 from contextlib import ExitStack
 
 import concourse.mybir as mybir
+from concourse.masks import make_identity
 
 D, T, I, Q, E, M = 512, 2048, 512, 512, 512, 1024
 FLOPS = 2 * D * Q * I + 2 * Q * E * I
@@ -18,6 +19,7 @@ P = 128
 PACK = 4
 HALF = I // 2
 RUN = 4
+SHARE = 128
 
 
 def tile_attend_keymiddle_delivered_lean_kernel(tc, query, keys, qs, msgs, old, fade, offs, offs2, offs3, offs4, out):
@@ -33,9 +35,10 @@ def tile_attend_keymiddle_delivered_lean_kernel(tc, query, keys, qs, msgs, old, 
         key_planes = [sb("keys%d" % t, [P, T], F32) for t in range(PACK)]
         keys_by_plane = keys.rearrange("(p t) n -> t p n", t=PACK)
         fade_all = sb("fade_all", [P, M], F32)
-        query_raw = [sb("query_raw%d" % u, [P, PACK, Q // 2], F32) for u in range(2)]
-        query_by_row = query.rearrange("(p t) q -> p t q", t=PACK)
-        msgs_raw = sb("msgs_raw", [P, PACK, E], F32)
+        fade_rows = sb("fade_rows", [P, 2, PACK], F32)
+        query_raw = sb("query_raw", [P, PACK, Q], F32)
+        msgs_raw = [sb("msgs_raw%d" % u, [P, PACK, E // 2], F32) for u in range(2)]
+        msgs_by_row = msgs.rearrange("(p r) e -> p r e", r=PACK)
         qs_rows = sb("qs_rows", [P, PACK], F32)
         contents = [sb("contents%d" % j, [P, M], F32) for j in range(E // P)]
 
@@ -44,19 +47,34 @@ def tile_attend_keymiddle_delivered_lean_kernel(tc, query, keys, qs, msgs, old, 
             nc.sync.dma_start(lists[n][:], src)
         for t in range(1, PACK):
             nc.sync.dma_start(out=key_planes[t][:], in_=keys_by_plane[t])
-            if t >= 2:
-                u = t - 2
-                nc.sync.dma_start(out=query_raw[u][:], in_=query_by_row[:, :, u * Q // 2 : (u + 1) * Q // 2])
-        nc.sync.dma_start(out=msgs_raw[:], in_=msgs.rearrange("(p r) e -> p r e", r=PACK))
+        nc.sync.dma_start(out=fade_rows[:], in_=fade.rearrange("o (h p c) -> (o p) h c", h=2, c=PACK))
+        nc.sync.dma_start(out=query_raw[:], in_=query.rearrange("(p t) q -> p t q", t=PACK))
+        for u in range(2):
+            nc.sync.dma_start(out=msgs_raw[u][:], in_=msgs_by_row[:, :, u * E // 2 : (u + 1) * E // 2])
         nc.sync.dma_start(out=qs_rows[:], in_=qs.rearrange("(p r) o -> p (r o)", r=PACK))
         nc.sync.dma_start(lists[3][:], offs4)
-        nc.sync.dma_start(out=fade_all[:], in_=fade[0].partition_broadcast(P))
         for j in range(E // P):
             nc.sync.dma_start(out=contents[j][:], in_=old[j * P : (j + 1) * P, :])
+            if j == 1:
+                nc.sync.dma_start(out=fade_all[:], in_=fade[0].partition_broadcast(P))
+
+        warm_in = sb("warm_in", [P, 1], F32)
+        warm_out = sb("warm_out", [P, 1], F32)
+        nc.gpsimd.memset(warm_in[:], 0.0)
+        nc.scalar.activation(warm_out[:], warm_in[:], ACT.Sigmoid)
 
         delivered = [sb("delivered%d" % j, [P, M], F32) for j in range(E // P)]
         for j in range(E // P):
             nc.vector.memset(delivered[j][:], 0.0)
+
+        ident = sb("ident", [P, P], F32)
+        make_identity(nc, ident[:])
+        fade_banks = []
+        for h in range(2):
+            bank = psum.tile([P, PACK, P], F32, name="fade_bank%d" % h)
+            for c in range(PACK):
+                nc.tensor.transpose(bank[:, c, :], fade_rows[:, h, c : c + 1].to_broadcast([P, P]), ident[:])
+            fade_banks.append(bank)
 
         low = sb("low", [P, PACK, I], F32)
         capped = sb("capped", [P, PACK, I], F32)
@@ -68,8 +86,8 @@ def tile_attend_keymiddle_delivered_lean_kernel(tc, query, keys, qs, msgs, old, 
             else:
                 nc.scalar.activation(got, window, ACT.Copy)
 
-        def narrow(t, lo, hi, a, b, c):
-            high = sb("high%d_%d" % (t, lo), [P, hi - lo], F32)
+        def narrow(t, lo, hi, a, b, c, tag=None):
+            high = sb("high%d_%d" % (t, lo), [P, hi - lo], F32, tag=tag)
             nc.vector.tensor_tensor(high[:], a, b, ALU.max)
             nc.vector.tensor_tensor(low[:, t, lo:hi], a, b, ALU.min)
             nc.vector.tensor_tensor(capped[:, t, lo:hi], high[:], c, ALU.min)
@@ -92,9 +110,9 @@ def tile_attend_keymiddle_delivered_lean_kernel(tc, query, keys, qs, msgs, old, 
             return quantize("zk%d" % h, zk[:], HALF)
 
         def scores(h, zk_mx, query_mx):
-            weights = sb("weights%d" % h, [P, HALF * PACK], F32)
+            weights = sb("weights%d" % h, [P, HALF * PACK], F32, tag="msgs_raw%d" % h)
             for u in range(2):
-                bank = psum.tile([P, PACK, P], F32, name="score_bank%d_%d" % (h, u))
+                bank = psum.tile([P, PACK, P], F32, name="score_bank%d_%d" % (h, u), tag="bank%d_%d" % (h, u))
                 cols = slice(u * P, (u + 1) * P)
                 for r in range(PACK):
                     rows = slice(r * P, (r + 1) * P)
@@ -115,7 +133,7 @@ def tile_attend_keymiddle_delivered_lean_kernel(tc, query, keys, qs, msgs, old, 
             return weights
 
         def weigh(h, weights, pieces):
-            wq = sb("wq%d" % h, [P, HALF * PACK], BF16)
+            wq = sb("wq%d" % h, [P, HALF * PACK], BF16, tag=("zk1", "zk0_codes")[h])
             width = HALF // pieces
             for u in range(pieces):
                 cols = slice(u * width * PACK, (u + 1) * width * PACK)
@@ -130,7 +148,7 @@ def tile_attend_keymiddle_delivered_lean_kernel(tc, query, keys, qs, msgs, old, 
         def carry(h, wq_mx, msgs_mx):
             banks = []
             for u in range(2):
-                bank = psum.tile([P, 2, HALF], F32, name="sum_bank%d_%d" % (h, u))
+                bank = psum.tile([P, 2, HALF], F32, name="sum_bank%d_%d" % (h, u), tag="bank%d_%d" % (h, u))
                 for jj in range(2):
                     rows = slice(jj * P, (jj + 1) * P)
                     nc.tensor.matmul_mx(
@@ -156,72 +174,84 @@ def tile_attend_keymiddle_delivered_lean_kernel(tc, query, keys, qs, msgs, old, 
         for t in range(last):
             got = [sb("got%d_%d" % (t, n), [P, I], F32) for n in range(3)]
             gather(False, 0, t, 0, I, got[0][:])
-            gather(t != 1, 1, t, 0, I, got[1][:])
+            if t == 0:
+                gather(False, 1, t, 0, HALF, got[1][:, :HALF])
+                gather(True, 1, t, HALF, I, got[1][:, HALF:])
+            else:
+                gather(False, 1, t, 0, I, got[1][:])
             gather(True, 2, t, 0, I, got[2][:])
             narrow(t, 0, I, got[0][:], got[1][:], got[2][:])
 
-        def last_plane(h):
-            got = [sb("got%d_%d_%d" % (last, n, h), [P, HALF], F32) for n in range(3)]
+        def last_plane(h, tag):
+            got = sb("got_last%d" % h, [P, 3, HALF], F32, tag=tag)
             for n in range(3):
-                gather(False, n, last, h * HALF, (h + 1) * HALF, got[n][:])
-            narrow(last, h * HALF, (h + 1) * HALF, got[0][:], got[1][:], got[2][:])
+                gather(False, n, last, h * HALF, (h + 1) * HALF, got[:, n, :])
+            narrow(last, h * HALF, (h + 1) * HALF, got[:, 0, :], got[:, 1, :], got[:, 2, :], (None, "zk0")[h])
             return middle(h)
 
-        zk_a = last_plane(0)
+        zk_a = last_plane(0, None)
         query_grouped = sb("query_grouped", [P, Q * PACK], BF16)
-        for u in range(2):
-            nc.scalar.copy(
-                out=query_grouped[:].rearrange("p (r u m t) -> p u m t r", r=PACK, u=2, t=PACK)[:, u],
-                in_=query_raw[u][:].rearrange("p t (m r) -> p m t r", r=PACK),
-            )
+        nc.scalar.copy(
+            out=query_grouped[:].rearrange("p (r m t) -> p m t r", r=PACK, t=PACK),
+            in_=query_raw[:].rearrange("p t (m r) -> p m t r", r=PACK),
+        )
         query_mx = quantize("query", query_grouped[:], Q)
-        weights_a = scores(0, zk_a, query_mx)
-        zk_b = last_plane(1)
-        wq_a = weigh(0, weights_a, 2)
-        weights_b = scores(1, zk_b, query_mx)
+        zk_b = last_plane(1, "query_raw")
 
-        msgs_mx = []
-        for u, tag in enumerate((None, "zk0_codes")):
-            msgs_grouped = sb("msgs_grouped%d" % u, [P, 2 * P * PACK], BF16, tag=tag)
+        def message_half(u, tag):
+            grouped = sb("msgs_grouped%d" % u, [P, 2 * P * PACK], BF16, tag=tag)
             for jj in range(2):
-                j = 2 * u + jj
                 nc.scalar.copy(
-                    out=msgs_grouped[:, jj * P * PACK : (jj + 1) * P * PACK].rearrange("p (c i r) -> p c r i", i=RUN, r=PACK),
-                    in_=msgs_raw[:, :, j * P : (j + 1) * P].rearrange("p r (c i) -> p c r i", i=RUN),
+                    out=grouped[:, jj * P * PACK : (jj + 1) * P * PACK].rearrange("p (c i r) -> p c r i", i=RUN, r=PACK),
+                    in_=msgs_raw[u][:, :, jj * P : (jj + 1) * P].rearrange("p r (c i) -> p c r i", i=RUN),
                 )
-            msgs_mx.append(quantize("msgs%d" % u, msgs_grouped[:], 2 * P))
+            return quantize("msgs%d" % u, grouped[:], 2 * P)
 
-        sums0 = sb("sums0", [P, I], F32)
+        msgs_mx = [message_half(0, "keys3")]
+        weights_a = scores(0, zk_a, query_mx)
+        msgs_mx.append(message_half(1, "zk0_codes"))
+        weights_b = scores(1, zk_b, query_mx)
+        wq_a = weigh(0, weights_a, 2)
+
         banks_a = carry(0, wq_a, msgs_mx)
-        sums1_a = sb("sums1_a", [P, HALF], F32)
-        sums23_a = sb("sums23_a", [P, 2, HALF], F32)
-        nc.scalar.copy(out=sums1_a[:], in_=banks_a[0][:, 1, :])
-        nc.scalar.copy(out=sums0[:, :HALF], in_=banks_a[0][:, 0, :])
-        nc.scalar.copy(out=sums23_a[:], in_=banks_a[1][:])
+        sums_a = [sb("sums_a%d" % u, [P, 2, HALF], F32) for u in range(2)]
+        for u in range(2):
+            nc.scalar.copy(out=sums_a[u][:], in_=banks_a[u][:])
+            for jj in ((0, 1), (1, 0))[u]:
+                deliver(False, 2 * u + jj, 0, HALF, sums_a[u][:, jj, :])
         wq_b = weigh(1, weights_b, 1)
         banks_b = carry(1, wq_b, msgs_mx)
-        sums1_b = sb("sums1_b", [P, HALF], F32)
-        sums23_b = sb("sums23_b", [P, 2, HALF], F32)
-        nc.vector.tensor_copy(out=sums0[:, HALF:], in_=banks_b[0][:, 0, :])
-        nc.vector.tensor_copy(out=sums1_b[:], in_=banks_b[0][:, 1, :])
-        nc.vector.tensor_copy(out=sums23_b[:], in_=banks_b[1][:])
-        deliver(False, 1, 0, HALF, sums1_a[:])
-        deliver(False, 0, 0, 128, sums0[:, :128])
-        for jj in range(2):
-            deliver(False, 2 + jj, 0, HALF, sums23_a[:, jj, :])
-        deliver(True, 0, 128, I, sums0[:, 128:])
-        deliver(False, 1, HALF, I, sums1_b[:])
-        for jj in range(2):
-            deliver(False, 2 + jj, HALF, I, sums23_b[:, jj, :])
+        sums_b = [sb("sums_b%d" % j, [P, HALF], F32) for j in range(2)]
+        sums_b23 = sb("sums_b23", [P, 2, HALF], F32)
+        for j in range(2):
+            nc.vector.tensor_copy(out=sums_b[j][:], in_=banks_b[0][:, j, :])
+        for j in range(2):
+            deliver(True, j, HALF, I, sums_b[j][:])
+        nc.vector.tensor_copy(out=sums_b23[:], in_=banks_b[1][:])
+        deliver(False, 2, HALF, I, sums_b23[:, 0, :])
+        deliver(True, 3, HALF, HALF + SHARE, sums_b23[:, 1, :SHARE])
+        deliver(False, 3, HALF + SHARE, I, sums_b23[:, 1, SHARE:])
 
-        fade_tags = ("weights0", "weights1", "sums0", "wq1_codes")
-        result_tags = (None, "weights0", None, None)
+        fade_tags = ("msgs_raw1", "zk0_codes", "sums_b0", "sums_b1")
+        faded = []
+        for j in range(E // P):
+            faded.append(sb("faded%d" % j, [P, M], F32, tag=fade_tags[j]))
+            if j == 1:
+                nc.gpsimd.tensor_tensor(faded[j][:], contents[j][:], fade_all[:], ALU.mult)
+                continue
+            for h in range(2):
+                cols = slice(h * M // 2, (h + 1) * M // 2)
+                nc.vector.tensor_tensor(
+                    faded[j][:, cols].rearrange("p (n c) -> p n c", c=PACK),
+                    contents[j][:, cols].rearrange("p (n c) -> p n c", c=PACK),
+                    fade_banks[h][:].rearrange("p c n -> p n c"),
+                    ALU.mult,
+                )
+        result_tags = (None, None, "zk0_codes", "sums_b0")
         for j, pieces in enumerate((1, 1, 2, 4)):
-            faded = sb("faded%d" % j, [P, M], F32, tag=fade_tags[j])
-            engine = nc.vector
-            engine.tensor_tensor(faded[:], contents[j][:], fade_all[:], ALU.mult)
+            engine = nc.gpsimd if j < 2 else nc.vector
             result = sb("result%d" % j, [P, M], F32, tag=result_tags[j])
             for u in range(pieces):
                 cols = slice(u * M // pieces, (u + 1) * M // pieces)
-                nc.vector.tensor_tensor(result[:, cols], faded[:, cols], delivered[j][:, cols], ALU.add)
+                engine.tensor_tensor(result[:, cols], faded[j][:, cols], delivered[j][:, cols], ALU.add)
                 nc.sync.dma_start(out=out[j * P : (j + 1) * P, cols], in_=result[:, cols])

@@ -19,7 +19,6 @@ P = 128
 PACK = 4
 HALF = I // 2
 RUN = 4
-SHARE = 128
 
 
 def tile_attend_keymiddle_delivered_lean_kernel(tc, query, keys, qs, msgs, old, fade, offs, offs2, offs3, offs4, out):
@@ -174,11 +173,7 @@ def tile_attend_keymiddle_delivered_lean_kernel(tc, query, keys, qs, msgs, old, 
         for t in range(last):
             got = [sb("got%d_%d" % (t, n), [P, I], F32) for n in range(3)]
             gather(False, 0, t, 0, I, got[0][:])
-            if t == 0:
-                gather(False, 1, t, 0, HALF, got[1][:, :HALF])
-                gather(True, 1, t, HALF, I, got[1][:, HALF:])
-            else:
-                gather(False, 1, t, 0, I, got[1][:])
+            gather(t == 0, 1, t, 0, I, got[1][:])
             gather(True, 2, t, 0, I, got[2][:])
             narrow(t, 0, I, got[0][:], got[1][:], got[2][:])
 
@@ -217,7 +212,7 @@ def tile_attend_keymiddle_delivered_lean_kernel(tc, query, keys, qs, msgs, old, 
         sums_a = [sb("sums_a%d" % u, [P, 2, HALF], F32) for u in range(2)]
         for u in range(2):
             nc.scalar.copy(out=sums_a[u][:], in_=banks_a[u][:])
-            for jj in ((0, 1), (1, 0))[u]:
+            for jj in range(2):
                 deliver(False, 2 * u + jj, 0, HALF, sums_a[u][:, jj, :])
         wq_b = weigh(1, weights_b, 1)
         banks_b = carry(1, wq_b, msgs_mx)
@@ -228,30 +223,40 @@ def tile_attend_keymiddle_delivered_lean_kernel(tc, query, keys, qs, msgs, old, 
         for j in range(2):
             deliver(True, j, HALF, I, sums_b[j][:])
         nc.vector.tensor_copy(out=sums_b23[:], in_=banks_b[1][:])
-        deliver(False, 2, HALF, I, sums_b23[:, 0, :])
-        deliver(True, 3, HALF, HALF + SHARE, sums_b23[:, 1, :SHARE])
-        deliver(False, 3, HALF + SHARE, I, sums_b23[:, 1, SHARE:])
+        for jj in range(2):
+            deliver(False, 2 + jj, HALF, I, sums_b23[:, jj, :])
 
-        fade_tags = ("msgs_raw1", "zk0_codes", "sums_b0", "sums_b1")
-        faded = []
-        for j in range(E // P):
-            faded.append(sb("faded%d" % j, [P, M], F32, tag=fade_tags[j]))
-            if j == 1:
-                nc.gpsimd.tensor_tensor(faded[j][:], contents[j][:], fade_all[:], ALU.mult)
-                continue
+        def fade_on_vector(j, tag):
+            faded = sb("faded%d" % j, [P, M], F32, tag=tag)
             for h in range(2):
                 cols = slice(h * M // 2, (h + 1) * M // 2)
                 nc.vector.tensor_tensor(
-                    faded[j][:, cols].rearrange("p (n c) -> p n c", c=PACK),
+                    faded[:, cols].rearrange("p (n c) -> p n c", c=PACK),
                     contents[j][:, cols].rearrange("p (n c) -> p n c", c=PACK),
                     fade_banks[h][:].rearrange("p c n -> p n c"),
                     ALU.mult,
                 )
-        result_tags = (None, None, "zk0_codes", "sums_b0")
-        for j, pieces in enumerate((1, 1, 2, 4)):
-            engine = nc.gpsimd if j < 2 else nc.vector
-            result = sb("result%d" % j, [P, M], F32, tag=result_tags[j])
+            return faded
+
+        def finish(engine, j, lo, faded, pieces, tag):
+            width = faded.shape[1]
+            result = sb("result%d_%d" % (j, lo), [P, width], F32, tag=tag)
             for u in range(pieces):
-                cols = slice(u * M // pieces, (u + 1) * M // pieces)
-                engine.tensor_tensor(result[:, cols], faded[j][:, cols], delivered[j][:, cols], ALU.add)
-                nc.sync.dma_start(out=out[j * P : (j + 1) * P, cols], in_=result[:, cols])
+                cols = slice(u * width // pieces, (u + 1) * width // pieces)
+                out_cols = slice(lo + cols.start, lo + cols.stop)
+                engine.tensor_tensor(result[:, cols], faded[:, cols], delivered[j][:, out_cols], ALU.add)
+                nc.sync.dma_start(out=out[j * P : (j + 1) * P, out_cols], in_=result[:, cols])
+
+        faded0 = fade_on_vector(0, "msgs_raw1")
+        faded1 = []
+        for h, tag in enumerate(("zk0_codes", "wq1_codes")):
+            cols = slice(h * M // 2, (h + 1) * M // 2)
+            faded1.append(sb("faded1_%d" % h, [P, M // 2], F32, tag=tag))
+            nc.gpsimd.tensor_tensor(faded1[h][:], contents[1][:, cols], fade_all[:, cols], ALU.mult)
+        faded2 = fade_on_vector(2, "sums_b0")
+        faded3 = fade_on_vector(3, "sums_b1")
+        finish(nc.gpsimd, 0, 0, faded0[:], 1, None)
+        finish(nc.gpsimd, 1, 0, faded1[0][:], 1, None)
+        finish(nc.vector, 1, M // 2, faded1[1][:], 1, "zk0_codes")
+        finish(nc.vector, 2, 0, faded2[:], 2, "wq1_codes")
+        finish(nc.vector, 3, 0, faded3[:], 4, "sums_b0")

from contextlib import ExitStack

import concourse.mybir as mybir
from concourse.masks import make_identity

D, T, I, Q, E, M = 512, 2048, 512, 512, 512, 1024
FLOPS = 2 * D * Q * I + 2 * Q * E * I

F32 = mybir.dt.float32
BF16 = mybir.dt.bfloat16
U32 = mybir.dt.uint32
U16 = mybir.dt.uint16
U8 = mybir.dt.uint8
FP8X4 = mybir.dt.float8_e4m3fn_x4
ALU = mybir.AluOpType
ACT = mybir.ActivationFunctionType

P = 128
PACK = 4
HALF = I // 2
RUN = 4


def tile_attend_keymiddle_delivered_lean_kernel(tc, query, keys, qs, msgs, old, fade, offs, offs2, offs3, offs4, out):
    nc = tc.nc
    with ExitStack() as ctx:
        held = ctx.enter_context(tc.tile_pool(name="held", bufs=1))
        psum = ctx.enter_context(tc.psum_pool(name="psum", bufs=1))

        def sb(name, shape, dtype, tag=None):
            return held.tile(shape, dtype, name=name, tag=tag or name, align_bytes=64)

        lists = [held.tile([P, I // 16], U16, name="list%d" % n) for n in range(4)]
        key_planes = [sb("keys%d" % t, [P, T], F32) for t in range(PACK)]
        keys_by_plane = keys.rearrange("(p t) n -> t p n", t=PACK)
        fade_all = sb("fade_all", [P, M], F32)
        fade_rows = sb("fade_rows", [P, 2, PACK], F32)
        query_raw = sb("query_raw", [P, PACK, Q], F32)
        msgs_raw = [sb("msgs_raw%d" % u, [P, PACK, E // 2], F32) for u in range(2)]
        msgs_by_row = msgs.rearrange("(p r) e -> p r e", r=PACK)
        qs_rows = sb("qs_rows", [P, PACK], F32)
        contents = [sb("contents%d" % j, [P, M], F32) for j in range(E // P)]

        nc.sync.dma_start(out=key_planes[0][:], in_=keys_by_plane[0])
        for n, src in enumerate((offs, offs2, offs3)):
            nc.sync.dma_start(lists[n][:], src)
        for t in range(1, PACK):
            nc.sync.dma_start(out=key_planes[t][:], in_=keys_by_plane[t])
        nc.sync.dma_start(out=fade_rows[:], in_=fade.rearrange("o (h p c) -> (o p) h c", h=2, c=PACK))
        nc.sync.dma_start(out=query_raw[:], in_=query.rearrange("(p t) q -> p t q", t=PACK))
        for u in range(2):
            nc.sync.dma_start(out=msgs_raw[u][:], in_=msgs_by_row[:, :, u * E // 2 : (u + 1) * E // 2])
        nc.sync.dma_start(out=qs_rows[:], in_=qs.rearrange("(p r) o -> p (r o)", r=PACK))
        nc.sync.dma_start(lists[3][:], offs4)
        for j in range(E // P):
            nc.sync.dma_start(out=contents[j][:], in_=old[j * P : (j + 1) * P, :])
            if j == 1:
                nc.sync.dma_start(out=fade_all[:], in_=fade[0].partition_broadcast(P))

        warm_in = sb("warm_in", [P, 1], F32)
        warm_out = sb("warm_out", [P, 1], F32)
        nc.gpsimd.memset(warm_in[:], 0.0)
        nc.scalar.activation(warm_out[:], warm_in[:], ACT.Sigmoid)

        delivered = [sb("delivered%d" % j, [P, M], F32) for j in range(E // P)]
        for j in range(E // P):
            nc.vector.memset(delivered[j][:], 0.0)

        ident = sb("ident", [P, P], F32)
        make_identity(nc, ident[:])
        fade_banks = []
        for h in range(2):
            bank = psum.tile([P, PACK, P], F32, name="fade_bank%d" % h)
            for c in range(PACK):
                nc.tensor.transpose(bank[:, c, :], fade_rows[:, h, c : c + 1].to_broadcast([P, P]), ident[:])
            fade_banks.append(bank)

        low = sb("low", [P, PACK, I], F32)
        capped = sb("capped", [P, PACK, I], F32)

        def gather(on_vector, n, t, lo, hi, got):
            window = key_planes[t][:].indirect(lists[n][:, lo // 16 : hi // 16])
            if on_vector:
                nc.vector.tensor_copy(got, window)
            else:
                nc.scalar.activation(got, window, ACT.Copy)

        def narrow(t, lo, hi, a, b, c, tag=None):
            high = sb("high%d_%d" % (t, lo), [P, hi - lo], F32, tag=tag)
            nc.vector.tensor_tensor(high[:], a, b, ALU.max)
            nc.vector.tensor_tensor(low[:, t, lo:hi], a, b, ALU.min)
            nc.vector.tensor_tensor(capped[:, t, lo:hi], high[:], c, ALU.min)

        def quantize(name, grouped, width):
            codes = sb(name + "_codes", [P, width], U32)
            scales = sb(name + "_scales", [P, width], U8)
            nc.vector.quantize_mx(out=codes[:].bitcast(FP8X4), scales=scales[:], in_=grouped)
            return codes, scales

        def middle(h):
            slots = slice(h * HALF, (h + 1) * HALF)
            zk = sb("zk%d" % h, [P, HALF * PACK], BF16)
            nc.vector.tensor_tensor(
                zk[:].rearrange("p (c i t) -> p c t i", i=RUN, t=PACK),
                low[:, :, slots].rearrange("p t (c i) -> p c t i", i=RUN),
                capped[:, :, slots].rearrange("p t (c i) -> p c t i", i=RUN),
                ALU.max,
            )
            return quantize("zk%d" % h, zk[:], HALF)

        def scores(h, zk_mx, query_mx):
            weights = sb("weights%d" % h, [P, HALF * PACK], F32, tag="msgs_raw%d" % h)
            for u in range(2):
                bank = psum.tile([P, PACK, P], F32, name="score_bank%d_%d" % (h, u), tag="bank%d_%d" % (h, u))
                cols = slice(u * P, (u + 1) * P)
                for r in range(PACK):
                    rows = slice(r * P, (r + 1) * P)
                    nc.tensor.matmul_mx(
                        out=bank[:, r, :],
                        lhsT=query_mx[0][:, rows].bitcast(FP8X4),
                        lhsT_scale=query_mx[1][:, rows],
                        rhs=zk_mx[0][:, cols].bitcast(FP8X4),
                        rhs_scale=zk_mx[1][:, cols],
                        start=True,
                        stop=True,
                    )
                nc.scalar.activation(
                    weights[:, u * P * PACK : (u + 1) * P * PACK].rearrange("p (n r) -> p n r", r=PACK),
                    bank[:].rearrange("p r n -> p n r"),
                    ACT.Sigmoid,
                )
            return weights

        def weigh(h, weights, pieces):
            wq = sb("wq%d" % h, [P, HALF * PACK], BF16, tag=("zk1", "zk0_codes")[h])
            width = HALF // pieces
            for u in range(pieces):
                cols = slice(u * width * PACK, (u + 1) * width * PACK)
                nc.vector.tensor_tensor(
                    wq[:, cols].rearrange("p (n r) -> p n r", r=PACK),
                    weights[:, cols].rearrange("p (n r) -> p n r", r=PACK),
                    qs_rows[:].unsqueeze(1).to_broadcast([P, width, PACK]),
                    ALU.mult,
                )
            return quantize("wq%d" % h, wq[:], HALF)

        def carry(h, wq_mx, msgs_mx):
            banks = []
            for u in range(2):
                bank = psum.tile([P, 2, HALF], F32, name="sum_bank%d_%d" % (h, u), tag="bank%d_%d" % (h, u))
                for jj in range(2):
                    rows = slice(jj * P, (jj + 1) * P)
                    nc.tensor.matmul_mx(
                        out=bank[:, jj, :],
                        lhsT=msgs_mx[u][0][:, rows].bitcast(FP8X4),
                        lhsT_scale=msgs_mx[u][1][:, rows],
                        rhs=wq_mx[0][:].bitcast(FP8X4),
                        rhs_scale=wq_mx[1][:],
                        start=True,
                        stop=True,
                    )
                banks.append(bank)
            return banks

        def deliver(on_vector, j, lo, hi, src):
            window = delivered[j][:].indirect(lists[3][:, lo // 16 : hi // 16])
            if on_vector:
                nc.vector.tensor_copy(window, src)
            else:
                nc.scalar.activation(window, src, ACT.Copy)

        last = PACK - 1
        for t in range(last):
            got = [sb("got%d_%d" % (t, n), [P, I], F32) for n in range(3)]
            gather(False, 0, t, 0, I, got[0][:])
            gather(t == 0, 1, t, 0, I, got[1][:])
            gather(True, 2, t, 0, I, got[2][:])
            narrow(t, 0, I, got[0][:], got[1][:], got[2][:])

        def last_plane(h, tag):
            got = sb("got_last%d" % h, [P, 3, HALF], F32, tag=tag)
            for n in range(3):
                gather(False, n, last, h * HALF, (h + 1) * HALF, got[:, n, :])
            narrow(last, h * HALF, (h + 1) * HALF, got[:, 0, :], got[:, 1, :], got[:, 2, :], (None, "zk0")[h])
            return middle(h)

        zk_a = last_plane(0, None)
        query_grouped = sb("query_grouped", [P, Q * PACK], BF16)
        nc.scalar.copy(
            out=query_grouped[:].rearrange("p (r m t) -> p m t r", r=PACK, t=PACK),
            in_=query_raw[:].rearrange("p t (m r) -> p m t r", r=PACK),
        )
        query_mx = quantize("query", query_grouped[:], Q)
        zk_b = last_plane(1, "query_raw")

        def message_half(u, tag):
            grouped = sb("msgs_grouped%d" % u, [P, 2 * P * PACK], BF16, tag=tag)
            for jj in range(2):
                nc.scalar.copy(
                    out=grouped[:, jj * P * PACK : (jj + 1) * P * PACK].rearrange("p (c i r) -> p c r i", i=RUN, r=PACK),
                    in_=msgs_raw[u][:, :, jj * P : (jj + 1) * P].rearrange("p r (c i) -> p c r i", i=RUN),
                )
            return quantize("msgs%d" % u, grouped[:], 2 * P)

        msgs_mx = [message_half(0, "keys3")]
        weights_a = scores(0, zk_a, query_mx)
        msgs_mx.append(message_half(1, "zk0_codes"))
        weights_b = scores(1, zk_b, query_mx)
        wq_a = weigh(0, weights_a, 2)

        banks_a = carry(0, wq_a, msgs_mx)
        sums_a = [sb("sums_a%d" % u, [P, 2, HALF], F32) for u in range(2)]
        for u in range(2):
            nc.scalar.copy(out=sums_a[u][:], in_=banks_a[u][:])
            for jj in range(2):
                deliver(False, 2 * u + jj, 0, HALF, sums_a[u][:, jj, :])
        wq_b = weigh(1, weights_b, 1)
        banks_b = carry(1, wq_b, msgs_mx)
        sums_b = [sb("sums_b%d" % j, [P, HALF], F32) for j in range(2)]
        sums_b23 = sb("sums_b23", [P, 2, HALF], F32)
        for j in range(2):
            nc.vector.tensor_copy(out=sums_b[j][:], in_=banks_b[0][:, j, :])
        for j in range(2):
            deliver(True, j, HALF, I, sums_b[j][:])
        nc.vector.tensor_copy(out=sums_b23[:], in_=banks_b[1][:])
        for jj in range(2):
            deliver(False, 2 + jj, HALF, I, sums_b23[:, jj, :])

        def fade_on_vector(j, tag):
            faded = sb("faded%d" % j, [P, M], F32, tag=tag)
            for h in range(2):
                cols = slice(h * M // 2, (h + 1) * M // 2)
                nc.vector.tensor_tensor(
                    faded[:, cols].rearrange("p (n c) -> p n c", c=PACK),
                    contents[j][:, cols].rearrange("p (n c) -> p n c", c=PACK),
                    fade_banks[h][:].rearrange("p c n -> p n c"),
                    ALU.mult,
                )
            return faded

        def finish(engine, j, lo, faded, pieces, tag):
            width = faded.shape[1]
            result = sb("result%d_%d" % (j, lo), [P, width], F32, tag=tag)
            for u in range(pieces):
                cols = slice(u * width // pieces, (u + 1) * width // pieces)
                out_cols = slice(lo + cols.start, lo + cols.stop)
                engine.tensor_tensor(result[:, cols], faded[:, cols], delivered[j][:, out_cols], ALU.add)
                nc.sync.dma_start(out=out[j * P : (j + 1) * P, out_cols], in_=result[:, cols])

        faded0 = fade_on_vector(0, "msgs_raw1")
        faded1 = []
        for h, tag in enumerate(("zk0_codes", "wq1_codes")):
            cols = slice(h * M // 2, (h + 1) * M // 2)
            faded1.append(sb("faded1_%d" % h, [P, M // 2], F32, tag=tag))
            nc.gpsimd.tensor_tensor(faded1[h][:], contents[1][:, cols], fade_all[:, cols], ALU.mult)
        faded2 = fade_on_vector(2, "sums_b0")
        faded3 = fade_on_vector(3, "sums_b1")
        finish(nc.gpsimd, 0, 0, faded0[:], 1, None)
        finish(nc.gpsimd, 1, 0, faded1[0][:], 1, None)
        finish(nc.vector, 1, M // 2, faded1[1][:], 1, "zk0_codes")
        finish(nc.vector, 2, 0, faded2[:], 2, "wq1_codes")
        finish(nc.vector, 3, 0, faded3[:], 4, "sums_b0")
